import numpy as np
import ml_dtypes


def mxq(x, axis, fmt="e4m3"):
    dtype, down = {"e4m3": (ml_dtypes.float8_e4m3fn, 7), "e5m2": (ml_dtypes.float8_e5m2, 14)}[fmt]
    v = np.moveaxis(np.asarray(x, np.float32).astype(ml_dtypes.bfloat16).astype(np.float64), axis, -1)
    blocks = v.reshape(v.shape[:-1] + (-1, 32))
    amax = np.abs(blocks).max(-1, keepdims=True)
    byte = np.maximum(np.where(amax > 0, np.frexp(amax)[1] - 1 + 127, 0) - down, 1)
    scale = np.exp2(byte - 127.0)
    codes = (blocks / scale).astype(np.float32).astype(dtype).astype(np.float64)
    return np.moveaxis((codes * scale).reshape(v.shape), -1, axis)


WIDE = False


def mx_kscale(k):
    if not WIDE:
        return np.ones(k)
    levels = np.array([10, -10, 5, -5, 0])
    if k % 512:
        return np.exp2(np.random.permutation(np.resize(levels, k // 32))).repeat(32)
    a = np.empty((k // 512, 16))
    for p in range(k // 512):
        a[p, :8] = np.random.permutation(np.resize(levels, 8))
        for g in range(8):
            far = levels[np.abs(levels - a[p, g]) >= 10]
            a[p, g + 8] = far[np.random.randint(len(far))]
    return np.exp2(a.ravel()).repeat(32)


def f64(x):
    return np.asarray(x).astype(np.float64)


def striped(idx):
    return np.tile(idx.reshape(-1, 16).T, (8, 1)).astype(np.uint16)


def unstriped(offs):
    return offs[:16].T.reshape(-1).astype(np.int64)


def striped8(idx):
    return np.concatenate([x.reshape(-1, 16).T for x in idx]).astype(np.uint16)


def runs(offs, k):
    lists = np.stack([offs[16 * r : 16 * r + 16].T.reshape(-1) for r in range(8)]).astype(np.int64)
    return lists[np.arange(k) % 512 // 64]


def pack_weight(w):
    k, n = w.shape
    w = f64(np.asarray(w, np.float32).astype(ml_dtypes.bfloat16)).reshape(k // 32, 32, n)
    amax = np.abs(w).max(1)
    byte = np.clip(np.where(amax > 0, np.frexp(amax)[1] - 1 + 127 - 7, 1), 1, 254)
    scaled = (w * np.exp2(127.0 - byte)[:, None, :]).reshape(k, n).astype(np.float32)
    words = np.ascontiguousarray(scaled.reshape(k // 512, 128, 4, n).transpose(0, 1, 3, 2)).astype(ml_dtypes.float8_e4m3fn).view(np.uint8)
    return words, np.ascontiguousarray(byte.astype(np.uint8).reshape(k // 512, 16, n))


def unpack_weight(words, scales):
    g, p, n, _ = words.shape
    vals = np.ascontiguousarray(words).view(ml_dtypes.float8_e4m3fn).astype(np.float64) * np.repeat(np.exp2(scales.astype(np.float64) - 127.0), 8, axis=1)[..., None]
    return vals.transpose(0, 1, 3, 2).reshape(g * 512, n)


K, T, S, H, C = 512, 2048, 512, 512, 512


def setup_inputs():
    n = np.random.standard_normal
    s = mx_kscale(K)[:, None]
    packed_xT = pack_weight(n((K, T)) * s)
    return {
        "x_words": packed_xT[0],
        "x_scales": packed_xT[1],
        "w1": (n((K, H)) / np.sqrt(K) / s).astype(np.float32),
        "gs": (np.random.uniform(0.5, 1.5, (K, 1)) / s).astype(np.float32),
        "gs2": (np.random.uniform(0.5, 1.5, (K, 1)) / s).astype(np.float32),
        "offs": striped(np.random.permutation(T)[:S]),
        "n1": striped(np.random.permutation(S)),
        "n2": striped(np.random.permutation(S)),
        "n3": striped8(np.stack([np.random.permutation(S) for _ in range(8)])),
        "n4": striped8(np.stack([np.random.permutation(S) for _ in range(8)])),
        "n5": striped8(np.stack([np.random.permutation(S) for _ in range(8)])),
        "n6": striped8(np.stack([np.random.permutation(S) for _ in range(8)])),
        "ca": striped(np.random.permutation(T)[:C]),
        "cb": striped(np.random.permutation(T)[:C]),
        "n7": striped8(np.stack([np.random.permutation(S) for _ in range(8)])),
        "n8": striped8(np.stack([np.random.permutation(S) for _ in range(8)])),
    }


def reference(x_words, x_scales, w1, gs, gs2, offs, n1, n2, n3, n4, n5, n6, ca, cb, n7, n8):
    x_ca = unpack_weight(x_words, x_scales)[:, unstriped(ca)]
    xq = unpack_weight(x_words, x_scales)[:, unstriped(offs)]
    y = mxq(f64(w1), 0, "e4m3").T @ xq
    sq = (y) ** 2
    z = f64(gs) * (y[:, unstriped(n2)] / (np.sqrt(sq + sq[:, unstriped(n1)] + 0.25)))
    a = 0.0625 * ((x_ca.T @ mxq(z, 0, "e4m3")))
    x_cb = unpack_weight(x_words, x_scales)[:, unstriped(cb)]
    z2 = f64(gs2) * (0.75 * ((y[np.arange(H)[:, None], runs(n3, H)]) * (y[np.arange(H)[:, None], runs(n4, H)]) - ((y[np.arange(H)[:, None], runs(n5, H)]) * (y[np.arange(H)[:, None], runs(n6, H)]))))
    b = 0.0625 * ((x_cb.T @ mxq(z2, 0, "e4m3")))
    return 0.75 * (a * (b[np.arange(C)[:, None], runs(n8, C)]) - ((a[np.arange(C)[:, None], runs(n7, C)]) * b))

@@ -1,0 +1,241 @@
+from contextlib import ExitStack
+
+import concourse.mybir as mybir
+from concourse.masks import make_identity
+
+K, T, S, H, C = 512, 2048, 512, 512, 512
+FLOPS = 2 * K * (H * S + 2 * C * S)
+
+F32 = mybir.dt.float32
+BF16 = mybir.dt.bfloat16
+I32 = mybir.dt.int32
+U32 = mybir.dt.uint32
+U16 = mybir.dt.uint16
+U8 = mybir.dt.uint8
+FP8X4 = mybir.dt.float8_e4m3fn_x4
+ALU = mybir.AluOpType
+ACT = mybir.ActivationFunctionType
+
+P = 128
+PACK = 4
+HALF = S // 2
+LIST_COLS = S // 16
+CFG = {"n2v":[3],"n5v":[0,1,2,3],"n3v":[],"early":0,"lz":1,"g1":1,"qh":4,"n8f":[0,1]}
+
+
+def tile_picked_twocdcrossbrmsdet_none_p_kernel(
+    tc, x_words, x_scales, w1, gs, gs2, offs, n1, n2, n3, n4, n5, n6, ca, cb, n7, n8, out
+):
+    nc = tc.nc
+    with ExitStack() as ctx:
+        keep = ctx.enter_context(tc.tile_pool(name="keep", bufs=1))
+        work = ctx.enter_context(tc.tile_pool(name="work", bufs=3))
+        psum = ctx.enter_context(tc.psum_pool(name="psum", bufs=1))
+
+        lists = {}
+
+        def load_list(name, source):
+            lists[name] = keep.tile([P, LIST_COLS], U16, name="list_" + name)
+            nc.sync.dma_start(lists[name][:], source)
+
+        def half_list(name, h):
+            return lists[name][:, h * LIST_COLS // 2 : (h + 1) * LIST_COLS // 2]
+
+        def cols(h):
+            return slice(h * HALF, (h + 1) * HALF)
+
+        xs = keep.tile([P, T], U8, name="xs", align_bytes=64)
+        for q in range(4):
+            rows = x_scales[0, 4 * q : 4 * q + 4, :].bitcast(I32)
+            nc.scalar.dma_start(xs[32 * q : 32 * (q + 1), :].bitcast(I32), rows.unsqueeze(0).to_broadcast([8, 4, T // 4]))
+        load_list("offs", offs)
+        load_list("ca", ca)
+        load_list("cb", cb)
+        w_raw = keep.tile([P, PACK, H], F32, name="w_raw")
+        nc.sync.dma_start(w_raw[:], w1.rearrange("(p j) c -> p j c", j=PACK))
+        xw = keep.tile([P, T], I32, name="xw", align_bytes=64)
+        nc.sync.dma_start(xw[:], x_words[0].rearrange("p n r -> p (n r)").bitcast(I32))
+        load_list("n1", n1)
+        gain = keep.tile([P, PACK], F32, name="gain")
+        nc.sync.dma_start(gain[:], gs.rearrange("(p t) o -> p (t o)", t=PACK))
+        load_list("n2", n2)
+        gain2 = keep.tile([P, PACK], F32, name="gain2")
+        nc.sync.dma_start(gain2[:], gs2.rearrange("(p t) o -> p (t o)", t=PACK))
+        for name, source in (("n3", n3), ("n4", n4), ("n5", n5), ("n6", n6), ("n7", n7), ("n8", n8)):
+            load_list(name, source)
+
+        xq_scales = keep.tile([P, S], U8, name="xq_scales", align_bytes=64)
+        nc.vector.tensor_copy(xq_scales[:], xs[:].indirect(lists["offs"][:]))
+        xq_words = keep.tile([P, S], U32, name="xq_words", align_bytes=64)
+        nc.vector.tensor_copy(xq_words[:], xw[:].bitcast(U32).indirect(lists["offs"][:]))
+
+        w_bf = keep.tile([P, PACK, P, PACK], BF16, name="w_bf", align_bytes=64)
+        nc.scalar.copy(w_bf[:].rearrange("p t m j -> p m j t"), w_raw[:].rearrange("p j (m t) -> p m j t", t=PACK))
+        w_words = keep.tile([P, PACK, P], U32, name="w_words", align_bytes=64)
+        w_scales = keep.tile([P, PACK, P], U8, name="w_scales", align_bytes=64)
+        y_banks = []
+        for t in range(PACK):
+            nc.vector.quantize_mx(
+                out=w_words[:, t, :].bitcast(FP8X4),
+                scales=w_scales[:, t, :],
+                in_=w_bf[:, t, :, :].rearrange("p m j -> p (m j)"),
+            )
+            bank = psum.tile([P, S], F32, name=f"first{t}")
+            nc.tensor.matmul_mx(
+                out=bank[:],
+                lhsT=w_words[:, t, :].bitcast(FP8X4),
+                lhsT_scale=w_scales[:, t, :],
+                rhs=xq_words[:].bitcast(FP8X4),
+                rhs_scale=xq_scales[:],
+                start=True,
+                stop=True,
+            )
+            y_banks.append(bank)
+
+        def pick_scoring(name):
+            words = keep.tile([P, PACK, C // 16, 4], U32, name=name + "_words", align_bytes=64)
+            nc.vector.tensor_copy(words[:].rearrange("p t a e -> p a t e"), xw[:].bitcast(U32).indirect(lists[name][:]))
+            picked = keep.tile([P, C], U8, name=name + "_picked", align_bytes=64)
+            nc.vector.tensor_copy(picked[:], xs[:].indirect(lists[name][:]))
+            scales = keep.tile([P, C], U8, name=name + "_scales", align_bytes=64)
+            nc.vector.tensor_copy(
+                scales[:].bitcast(I32).rearrange("p (t a) -> p t a", t=PACK),
+                picked[:].bitcast(I32).rearrange("p (a t) -> p t a", t=PACK),
+            )
+            return words, scales
+
+        ca_words, ca_scales = pick_scoring("ca")
+        cb_words, cb_scales = pick_scoring("cb")
+
+        def quantize_and_score(grouped, words, scales, targets, h, name):
+            z_words = keep.tile([P, HALF], U32, name=f"{name}_words{h}", align_bytes=64)
+            z_scales = keep.tile([P, HALF], U8, name=f"{name}_scales{h}", align_bytes=64)
+            nc.vector.quantize_mx(out=z_words[:].bitcast(FP8X4), scales=z_scales[:], in_=grouped[:])
+            for t in range(PACK):
+                nc.tensor.matmul_mx(
+                    out=targets[t],
+                    lhsT=words[:, t, :, :].rearrange("p a e -> p (a e)").bitcast(FP8X4),
+                    lhsT_scale=scales[:, t * P : (t + 1) * P],
+                    rhs=z_words[:].bitcast(FP8X4),
+                    rhs_scale=z_scales[:],
+                    start=True,
+                    stop=True,
+                )
+
+        def interleaved(grouped):
+            return grouped[:].rearrange("p (c i t) -> p c t i", i=4, t=PACK)
+
+        def planes(tile):
+            return tile[:].rearrange("p t (c i) -> p c t i", i=4)
+
+        identity = keep.tile([P, P], F32, name="identity")
+        make_identity(nc, identity[:])
+        y_sq = [keep.tile([P, 2 * S], F32, name=f"y_sq{t}") for t in range(PACK)]
+        yc_other = [keep.tile([P, 2 * S], F32, name=f"yc_other{t}") for t in range(PACK)]
+        a_f3 = [keep.tile([P, 2 * S], F32, name=f"a_f3{t}") for t in range(PACK)]
+        b_f5 = [keep.tile([P, 2 * S], F32, name=f"b_f5{t}") for t in range(PACK)]
+        z = keep.tile([P, PACK, S], F32, name="z")
+        right = keep.tile([P, PACK, S], F32, name="right")
+        low, high = slice(0, S), slice(S, 2 * S)
+
+        def halves(tile, h):
+            return tile[:, :, cols(h)].rearrange("p t (c i) -> p c t i", i=4)
+
+        def fetch(on_vector, target, looked_up):
+            if on_vector:
+                nc.vector.tensor_copy(target, looked_up)
+            else:
+                nc.scalar.activation(target, looked_up, ACT.Copy)
+
+        def y_out(t):
+            nc.scalar.activation(y_sq[t][:, high], y_banks[t][:], ACT.Square)
+            nc.scalar.copy(y_sq[t][:, low], y_banks[t][:])
+
+        turned = {}
+
+        def sum_squares(t):
+            for h in range(2):
+                nc.scalar.activation(
+                    yc_other[t][:, S + h * HALF : S + (h + 1) * HALF], y_sq[t][:, high].indirect(half_list("n1", h)), ACT.Copy
+                )
+            turned[t] = psum.tile([P, S], F32, name=f"second{2 * (t % 2)}")
+            for c in range(S // P):
+                block = slice(S + c * P, S + (c + 1) * P)
+                target = turned[t][:, c * P : (c + 1) * P]
+                nc.tensor.matmul(target, y_sq[t][:, block], identity[:], start=True, stop=False, is_transpose=True)
+                nc.tensor.matmul(target, yc_other[t][:, block], identity[:], start=False, stop=True, is_transpose=True)
+
+        def z_step(t):
+            picked = work.tile([P, S], F32, name="picked")
+            fetch(t in CFG["n2v"], picked[:], y_sq[t][:].indirect(lists["n2"][:]))
+            inv_turned = work.tile([P, S], F32, name="inv_turned")
+            nc.scalar.activation(inv_turned[:], turned[t][:], ACT.Abs_reciprocal_sqrt, bias=0.25)
+            inv = psum.tile([P, S], F32, name=f"second{2 * (t % 2) + 1}")
+            for c in range(S // P):
+                nc.tensor.transpose(inv[:, c * P : (c + 1) * P], inv_turned[:, c * P : (c + 1) * P], identity[:])
+            nc.vector.scalar_tensor_tensor(z[:, t, :], picked[:], gain[:, t : t + 1], inv[:], ALU.mult, ALU.mult)
+
+        def right_step(t):
+            nc.vector.tensor_scalar(yc_other[t][:, low], y_sq[t][:, low], gain2[:, t : t + 1], 0.75, ALU.mult, ALU.mult)
+            fetch(t in CFG["n5v"], b_f5[t][:, high], yc_other[t][:].indirect(lists["n5"][:]))
+            nc.vector.tensor_tensor(right[:, t, :], y_sq[t][:].indirect(lists["n6"][:]), b_f5[t][:, high], ALU.mult)
+
+        def left_step(t, left):
+            fetch(t in CFG["n3v"], a_f3[t][:, high], yc_other[t][:].indirect(lists["n3"][:]))
+            nc.vector.tensor_tensor(left[:, t, :], y_sq[t][:].indirect(lists["n4"][:]), a_f3[t][:, high], ALU.mult)
+
+        y_out(0)
+        sum_squares(0)
+        for t in range(PACK):
+            if t + 1 < PACK:
+                y_out(t + 1)
+                sum_squares(t + 1)
+            z_step(t)
+            right_step(t)
+            if t >= PACK - CFG["early"]:
+                pass
+
+        a_banks = [psum.tile([P, S], F32, name=f"first{t}") for t in range(PACK)]
+        z_grouped = [keep.tile([P, HALF * PACK], BF16, name=f"z_grouped{h}", align_bytes=64) for h in range(2)]
+        for h in range(2):
+            nc.vector.tensor_copy(interleaved(z_grouped[h]), halves(z, h))
+        for h in range(2):
+            quantize_and_score(z_grouped[h], ca_words, ca_scales, [bank[:, cols(h)] for bank in a_banks], h, "z")
+        left = keep.tile([P, PACK, S], F32, name="z" if CFG["lz"] else "left")
+        for t in range(PACK):
+            left_step(t, left)
+        for t in range(PACK):
+            nc.scalar.activation(a_f3[t][:, low], a_banks[t][:], ACT.Copy, scale=0.75 * 0.0625)
+
+        b_banks = [psum.tile([P, S], F32, name=f"second{t}") for t in range(PACK)]
+        for h in range(2):
+            z2_grouped = keep.tile([P, HALF * PACK], BF16, name="z2_grouped" if CFG["g1"] else f"z2_grouped{h}", align_bytes=64)
+            nc.vector.tensor_tensor(interleaved(z2_grouped), halves(left, h), halves(right, h), ALU.subtract)
+            b_parts = [b_banks[2 * h + t // 2][:, cols(t % 2)] for t in range(PACK)]
+            quantize_and_score(z2_grouped, cb_words, cb_scales, b_parts, h, "z2")
+            for t in range(PACK):
+                nc.scalar.activation(b_f5[t][:, cols(h)], b_parts[t], ACT.Copy, scale=0.0625)
+
+        out_rows = out.rearrange("(a t e) n -> t a e n", t=PACK, e=4)
+        a_picked = []
+        cross = []
+        for t in range(PACK):
+            picked = keep.tile([P, S], F32, name=f"a_picked{t}")
+            nc.scalar.activation(picked[:], a_f3[t][:].indirect(lists["n7"][:]), ACT.Copy)
+            a_picked.append(picked)
+            cross.append(keep.tile([P, S], F32, name=f"cross{t}"))
+            if t < CFG["qh"]:
+                nc.vector.tensor_tensor(cross[t][:, cols(0)], picked[:, cols(0)], b_f5[t][:, cols(0)], ALU.mult)
+        for t in range(PACK):
+            direct = work.tile([P, S], F32, name="direct")
+            if t in CFG["n8f"]:
+                nc.vector.tensor_tensor(direct[:], b_f5[t][:].indirect(lists["n8"][:]), a_f3[t][:, low], ALU.mult)
+            else:
+                b_picked = work.tile([P, S], F32, name="b_picked")
+                nc.scalar.activation(b_picked[:], b_f5[t][:].indirect(lists["n8"][:]), ACT.Copy)
+                nc.vector.tensor_tensor(direct[:], b_picked[:], a_f3[t][:, low], ALU.mult)
+            rest = cols(1) if t < CFG["qh"] else low
+            nc.vector.tensor_tensor(cross[t][:, rest], a_picked[t][:, rest], b_f5[t][:, rest], ALU.mult)
+            result = work.tile([P, S], F32, name="result")
+            nc.vector.tensor_tensor(result[:], direct[:], cross[t][:], ALU.subtract)
+            nc.sync.dma_start(out_rows[t], result[:])

@@ -20,7 +20,7 @@ P = 128
 PACK = 4
 HALF = S // 2
 LIST_COLS = S // 16
-CFG = {"n2v":[3],"n5v":[0,1,2,3],"n3v":[],"early":0,"lz":1,"g1":1,"qh":4,"n8f":[0,1]}
+CFG = {"n2v":[0,1,2],"n5v":[0,1],"n3v":[],"early":2,"n7v":[],"n8f":[0],"rg":[],"lz":1,"g1":1}
 
 
 def tile_picked_twocdcrossbrmsdet_none_p_kernel(
@@ -47,14 +47,17 @@ def tile_picked_twocdcrossbrmsdet_none_p_kernel(
         xs = keep.tile([P, T], U8, name="xs", align_bytes=64)
         for q in range(4):
             rows = x_scales[0, 4 * q : 4 * q + 4, :].bitcast(I32)
-            nc.scalar.dma_start(xs[32 * q : 32 * (q + 1), :].bitcast(I32), rows.unsqueeze(0).to_broadcast([8, 4, T // 4]))
+            nc.sync.dma_start(xs[32 * q : 32 * (q + 1), :].bitcast(I32), rows.unsqueeze(0).to_broadcast([8, 4, T // 4]))
         load_list("offs", offs)
         load_list("ca", ca)
         load_list("cb", cb)
-        w_raw = keep.tile([P, PACK, H], F32, name="w_raw")
-        nc.sync.dma_start(w_raw[:], w1.rearrange("(p j) c -> p j c", j=PACK))
         xw = keep.tile([P, T], I32, name="xw", align_bytes=64)
         nc.sync.dma_start(xw[:], x_words[0].rearrange("p n r -> p (n r)").bitcast(I32))
+        w_raw = []
+        for v in range(2):
+            raw = keep.tile([P, PACK, H // 2], F32, name=f"w_raw{v}")
+            nc.sync.dma_start(raw[:], w1[:, v * H // 2 : (v + 1) * H // 2].rearrange("(p j) c -> p j c", j=PACK))
+            w_raw.append(raw)
         load_list("n1", n1)
         gain = keep.tile([P, PACK], F32, name="gain")
         nc.sync.dma_start(gain[:], gs.rearrange("(p t) o -> p (t o)", t=PACK))
@@ -64,22 +67,34 @@ def tile_picked_twocdcrossbrmsdet_none_p_kernel(
         for name, source in (("n3", n3), ("n4", n4), ("n5", n5), ("n6", n6), ("n7", n7), ("n8", n8)):
             load_list(name, source)
 
+        warm = keep.tile([P, 1], F32, name="warm")
+        nc.vector.memset(warm[:], 1.0)
+        nc.scalar.activation(warm[:], warm[:], ACT.Abs_reciprocal_sqrt)
         xq_scales = keep.tile([P, S], U8, name="xq_scales", align_bytes=64)
         nc.vector.tensor_copy(xq_scales[:], xs[:].indirect(lists["offs"][:]))
         xq_words = keep.tile([P, S], U32, name="xq_words", align_bytes=64)
         nc.vector.tensor_copy(xq_words[:], xw[:].bitcast(U32).indirect(lists["offs"][:]))
 
-        w_bf = keep.tile([P, PACK, P, PACK], BF16, name="w_bf", align_bytes=64)
-        nc.scalar.copy(w_bf[:].rearrange("p t m j -> p m j t"), w_raw[:].rearrange("p j (m t) -> p m j t", t=PACK))
+        w_bf = [keep.tile([P, 2, P, PACK], BF16, name=f"w_bf{u}", align_bytes=64) for u in range(2)]
+        for v in range(2):
+            for u in range(2):
+                columns = w_raw[v][:].rearrange("p j (m t) -> p m j t", t=PACK)[:, :, :, 2 * u : 2 * u + 2]
+                nc.scalar.copy(w_bf[u][:, :, v * P // 2 : (v + 1) * P // 2, :].rearrange("p t m j -> p m j t"), columns)
         w_words = keep.tile([P, PACK, P], U32, name="w_words", align_bytes=64)
         w_scales = keep.tile([P, PACK, P], U8, name="w_scales", align_bytes=64)
-        y_banks = []
-        for t in range(PACK):
+        def quantize_w(t):
             nc.vector.quantize_mx(
                 out=w_words[:, t, :].bitcast(FP8X4),
                 scales=w_scales[:, t, :],
-                in_=w_bf[:, t, :, :].rearrange("p m j -> p (m j)"),
+                in_=w_bf[t // 2][:, t % 2, :, :].rearrange("p m j -> p (m j)"),
             )
+
+        quantize_w(0)
+        quantize_w(1)
+        quantize_w(2)
+        quantize_w(3)
+        y_banks = []
+        for t in range(PACK):
             bank = psum.tile([P, S], F32, name=f"first{t}")
             nc.tensor.matmul_mx(
                 out=bank[:],
@@ -92,8 +107,8 @@ def tile_picked_twocdcrossbrmsdet_none_p_kernel(
             )
             y_banks.append(bank)
 
-        def pick_scoring(name):
-            words = keep.tile([P, PACK, C // 16, 4], U32, name=name + "_words", align_bytes=64)
+        def pick_scoring(name, slot):
+            words = keep.tile([P, PACK, C // 16, 4], U32, name=name + "_words", tag=slot, align_bytes=64)
             nc.vector.tensor_copy(words[:].rearrange("p t a e -> p a t e"), xw[:].bitcast(U32).indirect(lists[name][:]))
             picked = keep.tile([P, C], U8, name=name + "_picked", align_bytes=64)
             nc.vector.tensor_copy(picked[:], xs[:].indirect(lists[name][:]))
@@ -104,8 +119,8 @@ def tile_picked_twocdcrossbrmsdet_none_p_kernel(
             )
             return words, scales
 
-        ca_words, ca_scales = pick_scoring("ca")
-        cb_words, cb_scales = pick_scoring("cb")
+        ca_words, ca_scales = pick_scoring("ca", "w_bf0")
+        cb_words, cb_scales = pick_scoring("cb", "w_bf1")
 
         def quantize_and_score(grouped, words, scales, targets, h, name):
             z_words = keep.tile([P, HALF], U32, name=f"{name}_words{h}", align_bytes=64)
@@ -176,7 +191,6 @@ def tile_picked_twocdcrossbrmsdet_none_p_kernel(
             nc.vector.scalar_tensor_tensor(z[:, t, :], picked[:], gain[:, t : t + 1], inv[:], ALU.mult, ALU.mult)
 
         def right_step(t):
-            nc.vector.tensor_scalar(yc_other[t][:, low], y_sq[t][:, low], gain2[:, t : t + 1], 0.75, ALU.mult, ALU.mult)
             fetch(t in CFG["n5v"], b_f5[t][:, high], yc_other[t][:].indirect(lists["n5"][:]))
             nc.vector.tensor_tensor(right[:, t, :], y_sq[t][:].indirect(lists["n6"][:]), b_f5[t][:, high], ALU.mult)
 
@@ -191,9 +205,9 @@ def tile_picked_twocdcrossbrmsdet_none_p_kernel(
                 y_out(t + 1)
                 sum_squares(t + 1)
             z_step(t)
-            right_step(t)
-            if t >= PACK - CFG["early"]:
-                pass
+            nc.vector.tensor_scalar(yc_other[t][:, low], y_sq[t][:, low], gain2[:, t : t + 1], 0.75, ALU.mult, ALU.mult)
+            if t < CFG["early"]:
+                right_step(t)
 
         a_banks = [psum.tile([P, S], F32, name=f"first{t}") for t in range(PACK)]
         z_grouped = [keep.tile([P, HALF * PACK], BF16, name=f"z_grouped{h}", align_bytes=64) for h in range(2)]
@@ -203,29 +217,33 @@ def tile_picked_twocdcrossbrmsdet_none_p_kernel(
             quantize_and_score(z_grouped[h], ca_words, ca_scales, [bank[:, cols(h)] for bank in a_banks], h, "z")
         left = keep.tile([P, PACK, S], F32, name="z" if CFG["lz"] else "left")
         for t in range(PACK):
+            if t >= CFG["early"]:
+                right_step(t)
             left_step(t, left)
         for t in range(PACK):
             nc.scalar.activation(a_f3[t][:, low], a_banks[t][:], ACT.Copy, scale=0.75 * 0.0625)
 
+        b_parts = {}
         b_banks = [psum.tile([P, S], F32, name=f"second{t}") for t in range(PACK)]
         for h in range(2):
             z2_grouped = keep.tile([P, HALF * PACK], BF16, name="z2_grouped" if CFG["g1"] else f"z2_grouped{h}", align_bytes=64)
             nc.vector.tensor_tensor(interleaved(z2_grouped), halves(left, h), halves(right, h), ALU.subtract)
-            b_parts = [b_banks[2 * h + t // 2][:, cols(t % 2)] for t in range(PACK)]
-            quantize_and_score(z2_grouped, cb_words, cb_scales, b_parts, h, "z2")
+            b_parts[h] = [b_banks[2 * h + t // 2][:, cols(t % 2)] for t in range(PACK)]
+            quantize_and_score(z2_grouped, cb_words, cb_scales, b_parts[h], h, "z2")
             for t in range(PACK):
-                nc.scalar.activation(b_f5[t][:, cols(h)], b_parts[t], ACT.Copy, scale=0.0625)
+                nc.scalar.activation(b_f5[t][:, cols(h)], b_parts[h][t], ACT.Copy, scale=0.0625)
 
         out_rows = out.rearrange("(a t e) n -> t a e n", t=PACK, e=4)
         a_picked = []
         cross = []
         for t in range(PACK):
             picked = keep.tile([P, S], F32, name=f"a_picked{t}")
-            nc.scalar.activation(picked[:], a_f3[t][:].indirect(lists["n7"][:]), ACT.Copy)
+            fetch(t in CFG["n7v"], picked[:], a_f3[t][:].indirect(lists["n7"][:]))
             a_picked.append(picked)
             cross.append(keep.tile([P, S], F32, name=f"cross{t}"))
-            if t < CFG["qh"]:
-                nc.vector.tensor_tensor(cross[t][:, cols(0)], picked[:, cols(0)], b_f5[t][:, cols(0)], ALU.mult)
+        for h in range(2):
+            for t in range(PACK):
+                nc.vector.scalar_tensor_tensor(cross[t][:, cols(h)], b_parts[h][t], 0.0625, a_picked[t][:, cols(h)], ALU.mult, ALU.mult)
         for t in range(PACK):
             direct = work.tile([P, S], F32, name="direct")
             if t in CFG["n8f"]:
@@ -233,9 +251,7 @@ def tile_picked_twocdcrossbrmsdet_none_p_kernel(
             else:
                 b_picked = work.tile([P, S], F32, name="b_picked")
                 nc.scalar.activation(b_picked[:], b_f5[t][:].indirect(lists["n8"][:]), ACT.Copy)
-                nc.vector.tensor_tensor(direct[:], b_picked[:], a_f3[t][:, low], ALU.mult)
-            rest = cols(1) if t < CFG["qh"] else low
-            nc.vector.tensor_tensor(cross[t][:, rest], a_picked[t][:, rest], b_f5[t][:, rest], ALU.mult)
-            result = work.tile([P, S], F32, name="result")
-            nc.vector.tensor_tensor(result[:], direct[:], cross[t][:], ALU.subtract)
+                nc.vector.scalar_tensor_tensor(direct[:], a_banks[t][:], 0.75 * 0.0625, b_picked[:], ALU.mult, ALU.mult)
+            result = work.tile([P, S], F32, name="result", bufs=4)
+            (nc.gpsimd if t in CFG["rg"] else nc.vector).tensor_tensor(result[:], direct[:], cross[t][:], ALU.subtract)
             nc.sync.dma_start(out_rows[t], result[:])

@@ -20,7 +20,7 @@ P = 128
 PACK = 4
 HALF = S // 2
 LIST_COLS = S // 16
-CFG = {"n2v":[0,1,2],"n5v":[0,1],"n3v":[],"early":2,"n7v":[],"n8f":[0],"rg":[],"lz":1,"g1":1}
+CFG = {"n2v":[0,1],"n5v":[0,1,2],"n3v":[],"early":3,"n7v":[],"n8f":[0],"rg":[],"lz":1,"g1":0,"aa":[],"pk":0,"dg":[],"hl":[3],"de":1,"kf":0,"ll":0,"ca":-1,"cb":-1,"sh":[3],"jh":3}
 
 
 def tile_picked_twocdcrossbrmsdet_none_p_kernel(
@@ -107,20 +107,20 @@ def tile_picked_twocdcrossbrmsdet_none_p_kernel(
             )
             y_banks.append(bank)
 
-        def pick_scoring(name, slot):
-            words = keep.tile([P, PACK, C // 16, 4], U32, name=name + "_words", tag=slot, align_bytes=64)
-            nc.vector.tensor_copy(words[:].rearrange("p t a e -> p a t e"), xw[:].bitcast(U32).indirect(lists[name][:]))
+        dealt = {}
+        for name in ("ca", "cb"):
             picked = keep.tile([P, C], U8, name=name + "_picked", align_bytes=64)
             nc.vector.tensor_copy(picked[:], xs[:].indirect(lists[name][:]))
-            scales = keep.tile([P, C], U8, name=name + "_scales", align_bytes=64)
+            dealt[name] = keep.tile([P, C], U8, name=name + "_scales", align_bytes=64)
             nc.vector.tensor_copy(
-                scales[:].bitcast(I32).rearrange("p (t a) -> p t a", t=PACK),
+                dealt[name][:].bitcast(I32).rearrange("p (t a) -> p t a", t=PACK),
                 picked[:].bitcast(I32).rearrange("p (a t) -> p t a", t=PACK),
             )
-            return words, scales
 
-        ca_words, ca_scales = pick_scoring("ca", "w_bf0")
-        cb_words, cb_scales = pick_scoring("cb", "w_bf1")
+        def pick_words(name, slot):
+            words = keep.tile([P, PACK, C // 16, 4], U32, name=name + "_words", tag=slot, align_bytes=64)
+            nc.vector.tensor_copy(words[:].rearrange("p t a e -> p a t e"), xw[:].bitcast(U32).indirect(lists[name][:]))
+            return words, dealt[name]
 
         def quantize_and_score(grouped, words, scales, targets, h, name):
             z_words = keep.tile([P, HALF], U32, name=f"{name}_words{h}", align_bytes=64)
@@ -164,7 +164,8 @@ def tile_picked_twocdcrossbrmsdet_none_p_kernel(
 
         def y_out(t):
             nc.scalar.activation(y_sq[t][:, high], y_banks[t][:], ACT.Square)
-            nc.scalar.copy(y_sq[t][:, low], y_banks[t][:])
+            if t not in CFG["aa"]:
+                nc.scalar.copy(y_sq[t][:, low], y_banks[t][:])
 
         turned = {}
 
@@ -173,6 +174,8 @@ def tile_picked_twocdcrossbrmsdet_none_p_kernel(
                 nc.scalar.activation(
                     yc_other[t][:, S + h * HALF : S + (h + 1) * HALF], y_sq[t][:, high].indirect(half_list("n1", h)), ACT.Copy
                 )
+            if t in CFG["aa"]:
+                nc.scalar.copy(y_sq[t][:, low], y_banks[t][:])
             turned[t] = psum.tile([P, S], F32, name=f"second{2 * (t % 2)}")
             for c in range(S // P):
                 block = slice(S + c * P, S + (c + 1) * P)
@@ -181,33 +184,67 @@ def tile_picked_twocdcrossbrmsdet_none_p_kernel(
                 nc.tensor.matmul(target, yc_other[t][:, block], identity[:], start=False, stop=True, is_transpose=True)
 
         def z_step(t):
-            picked = work.tile([P, S], F32, name="picked")
-            fetch(t in CFG["n2v"], picked[:], y_sq[t][:].indirect(lists["n2"][:]))
+            picked = right[:, CFG["early"], :] if t == 3 and CFG["pk"] else work.tile([P, S], F32, name="picked")[:]
+            fetch(t in CFG["n2v"], picked, y_sq[t][:].indirect(lists["n2"][:]))
             inv_turned = work.tile([P, S], F32, name="inv_turned")
             nc.scalar.activation(inv_turned[:], turned[t][:], ACT.Abs_reciprocal_sqrt, bias=0.25)
             inv = psum.tile([P, S], F32, name=f"second{2 * (t % 2) + 1}")
             for c in range(S // P):
                 nc.tensor.transpose(inv[:, c * P : (c + 1) * P], inv_turned[:, c * P : (c + 1) * P], identity[:])
-            nc.vector.scalar_tensor_tensor(z[:, t, :], picked[:], gain[:, t : t + 1], inv[:], ALU.mult, ALU.mult)
+            for part in ([cols(0), cols(1)] if t in CFG["sh"] else [low]):
+                nc.vector.scalar_tensor_tensor(z[:, t, part], picked[:, part], gain[:, t : t + 1], inv[:, part], ALU.mult, ALU.mult)
 
         def right_step(t):
+            right_fetch(t)
+            right_mult(t)
+
+        def right_fetch(t):
             fetch(t in CFG["n5v"], b_f5[t][:, high], yc_other[t][:].indirect(lists["n5"][:]))
-            nc.vector.tensor_tensor(right[:, t, :], y_sq[t][:].indirect(lists["n6"][:]), b_f5[t][:, high], ALU.mult)
+
+        def right_mult(t, part=low):
+            offsets = lists["n6"][:, part.start // 16 : part.stop // 16]
+            nc.vector.tensor_tensor(right[:, t, part], y_sq[t][:].indirect(offsets), b_f5[t][:, high][:, part], ALU.mult)
+
+        def left_mult(t, left, part=low):
+            offsets = lists["n4"][:, part.start // 16 : part.stop // 16]
+            nc.vector.tensor_tensor(left[:, t, part], y_sq[t][:].indirect(offsets), a_f3[t][:, high][:, part], ALU.mult)
 
         def left_step(t, left):
             fetch(t in CFG["n3v"], a_f3[t][:, high], yc_other[t][:].indirect(lists["n3"][:]))
-            nc.vector.tensor_tensor(left[:, t, :], y_sq[t][:].indirect(lists["n4"][:]), a_f3[t][:, high], ALU.mult)
 
+        def weigh(t):
+            nc.vector.tensor_scalar(yc_other[t][:, low], y_sq[t][:, low], gain2[:, t : t + 1], 0.75, ALU.mult, ALU.mult)
+
+        if CFG["ca"] < 0:
+            ca_words, ca_scales = pick_words("ca", "w_bf0")
+        if CFG["cb"] < 0:
+            cb_words, cb_scales = pick_words("cb", "w_bf1")
         y_out(0)
         sum_squares(0)
+        if CFG["de"]:
+            weigh(0)
         for t in range(PACK):
             if t + 1 < PACK:
                 y_out(t + 1)
                 sum_squares(t + 1)
+                if CFG["de"]:
+                    weigh(t + 1)
+            if CFG["kf"] and t < CFG["early"]:
+                right_fetch(t)
             z_step(t)
-            nc.vector.tensor_scalar(yc_other[t][:, low], y_sq[t][:, low], gain2[:, t : t + 1], 0.75, ALU.mult, ALU.mult)
+            if not CFG["de"]:
+                weigh(t)
+            if CFG["ll"] and 0 < t <= CFG["early"]:
+                right_mult(t - 1)
             if t < CFG["early"]:
-                right_step(t)
+                if not CFG["kf"]:
+                    right_fetch(t)
+                if not CFG["ll"]:
+                    right_mult(t)
+            if t == CFG["ca"]:
+                ca_words, ca_scales = pick_words("ca", "w_bf0")
+            if t == CFG["cb"]:
+                cb_words, cb_scales = pick_words("cb", "w_bf1")
 
         a_banks = [psum.tile([P, S], F32, name=f"first{t}") for t in range(PACK)]
         z_grouped = [keep.tile([P, HALF * PACK], BF16, name=f"z_grouped{h}", align_bytes=64) for h in range(2)]
@@ -218,14 +255,22 @@ def tile_picked_twocdcrossbrmsdet_none_p_kernel(
         left = keep.tile([P, PACK, S], F32, name="z" if CFG["lz"] else "left")
         for t in range(PACK):
             if t >= CFG["early"]:
-                right_step(t)
+                right_fetch(t)
+                if t < CFG["jh"]:
+                    right_mult(t)
             left_step(t, left)
+            if t < CFG["jh"]:
+                left_mult(t, left)
         for t in range(PACK):
             nc.scalar.activation(a_f3[t][:, low], a_banks[t][:], ACT.Copy, scale=0.75 * 0.0625)
 
         b_parts = {}
         b_banks = [psum.tile([P, S], F32, name=f"second{t}") for t in range(PACK)]
         for h in range(2):
+            for t in range(CFG["jh"], PACK):
+                if t >= CFG["early"]:
+                    right_mult(t, cols(h))
+                left_mult(t, left, cols(h))
             z2_grouped = keep.tile([P, HALF * PACK], BF16, name="z2_grouped" if CFG["g1"] else f"z2_grouped{h}", align_bytes=64)
             nc.vector.tensor_tensor(interleaved(z2_grouped), halves(left, h), halves(right, h), ALU.subtract)
             b_parts[h] = [b_banks[2 * h + t // 2][:, cols(t % 2)] for t in range(PACK)]
@@ -245,13 +290,16 @@ def tile_picked_twocdcrossbrmsdet_none_p_kernel(
             for t in range(PACK):
                 nc.vector.scalar_tensor_tensor(cross[t][:, cols(h)], b_parts[h][t], 0.0625, a_picked[t][:, cols(h)], ALU.mult, ALU.mult)
         for t in range(PACK):
-            direct = work.tile([P, S], F32, name="direct")
-            if t in CFG["n8f"]:
-                nc.vector.tensor_tensor(direct[:], b_f5[t][:].indirect(lists["n8"][:]), a_f3[t][:, low], ALU.mult)
-            else:
-                b_picked = work.tile([P, S], F32, name="b_picked")
-                nc.scalar.activation(b_picked[:], b_f5[t][:].indirect(lists["n8"][:]), ACT.Copy)
-                nc.vector.scalar_tensor_tensor(direct[:], a_banks[t][:], 0.75 * 0.0625, b_picked[:], ALU.mult, ALU.mult)
-            result = work.tile([P, S], F32, name="result", bufs=4)
-            (nc.gpsimd if t in CFG["rg"] else nc.vector).tensor_tensor(result[:], direct[:], cross[t][:], ALU.subtract)
-            nc.sync.dma_start(out_rows[t], result[:])
+            for part in ([cols(0), cols(1)] if t in CFG["hl"] else [low]):
+                width = part.stop - part.start
+                offsets = lists["n8"][:, part.start // 16 : part.stop // 16]
+                direct = work.tile([P, width], F32, name="direct")
+                if t in CFG["n8f"]:
+                    nc.vector.tensor_tensor(direct[:], b_f5[t][:].indirect(offsets), a_f3[t][:, part], ALU.mult)
+                else:
+                    b_picked = work.tile([P, width], F32, name="b_picked", bufs=4)
+                    nc.scalar.activation(b_picked[:], b_f5[t][:].indirect(offsets), ACT.Copy)
+                    nc.vector.scalar_tensor_tensor(direct[:], a_banks[t][:, part], 0.75 * 0.0625, b_picked[:], ALU.mult, ALU.mult)
+                result = work.tile([P, width], F32, name="result", bufs=5)
+                (nc.gpsimd if t in CFG["rg"] else nc.vector).tensor_tensor(result[:], direct[:], cross[t][:, part], ALU.subtract)
+                nc.sync.dma_start(out_rows[t][:, :, part], result[:])

from contextlib import ExitStack

import concourse.mybir as mybir
from concourse.masks import make_identity

K, T, S, H, C = 512, 2048, 512, 512, 512
FLOPS = 2 * K * (H * S + 2 * C * S)

F32 = mybir.dt.float32
BF16 = mybir.dt.bfloat16
I32 = mybir.dt.int32
U32 = mybir.dt.uint32
U16 = mybir.dt.uint16
U8 = mybir.dt.uint8
FP8X4 = mybir.dt.float8_e4m3fn_x4
ALU = mybir.AluOpType
ACT = mybir.ActivationFunctionType

P = 128
PACK = 4
HALF = S // 2
LIST_COLS = S // 16
CFG = {"n2v":[0,1],"n5v":[0,1,2],"n3v":[],"early":3,"n7v":[],"n8f":[0],"rg":[],"lz":1,"g1":0,"aa":[],"pk":0,"dg":[],"hl":[3],"de":1,"kf":0,"ll":0,"ca":-1,"cb":-1,"sh":[3],"jh":3}


def tile_picked_twocdcrossbrmsdet_none_p_kernel(
    tc, x_words, x_scales, w1, gs, gs2, offs, n1, n2, n3, n4, n5, n6, ca, cb, n7, n8, out
):
    nc = tc.nc
    with ExitStack() as ctx:
        keep = ctx.enter_context(tc.tile_pool(name="keep", bufs=1))
        work = ctx.enter_context(tc.tile_pool(name="work", bufs=3))
        psum = ctx.enter_context(tc.psum_pool(name="psum", bufs=1))

        lists = {}

        def load_list(name, source):
            lists[name] = keep.tile([P, LIST_COLS], U16, name="list_" + name)
            nc.sync.dma_start(lists[name][:], source)

        def half_list(name, h):
            return lists[name][:, h * LIST_COLS // 2 : (h + 1) * LIST_COLS // 2]

        def cols(h):
            return slice(h * HALF, (h + 1) * HALF)

        xs = keep.tile([P, T], U8, name="xs", align_bytes=64)
        for q in range(4):
            rows = x_scales[0, 4 * q : 4 * q + 4, :].bitcast(I32)
            nc.sync.dma_start(xs[32 * q : 32 * (q + 1), :].bitcast(I32), rows.unsqueeze(0).to_broadcast([8, 4, T // 4]))
        load_list("offs", offs)
        load_list("ca", ca)
        load_list("cb", cb)
        xw = keep.tile([P, T], I32, name="xw", align_bytes=64)
        nc.sync.dma_start(xw[:], x_words[0].rearrange("p n r -> p (n r)").bitcast(I32))
        w_raw = []
        for v in range(2):
            raw = keep.tile([P, PACK, H // 2], F32, name=f"w_raw{v}")
            nc.sync.dma_start(raw[:], w1[:, v * H // 2 : (v + 1) * H // 2].rearrange("(p j) c -> p j c", j=PACK))
            w_raw.append(raw)
        load_list("n1", n1)
        gain = keep.tile([P, PACK], F32, name="gain")
        nc.sync.dma_start(gain[:], gs.rearrange("(p t) o -> p (t o)", t=PACK))
        load_list("n2", n2)
        gain2 = keep.tile([P, PACK], F32, name="gain2")
        nc.sync.dma_start(gain2[:], gs2.rearrange("(p t) o -> p (t o)", t=PACK))
        for name, source in (("n3", n3), ("n4", n4), ("n5", n5), ("n6", n6), ("n7", n7), ("n8", n8)):
            load_list(name, source)

        warm = keep.tile([P, 1], F32, name="warm")
        nc.vector.memset(warm[:], 1.0)
        nc.scalar.activation(warm[:], warm[:], ACT.Abs_reciprocal_sqrt)
        xq_scales = keep.tile([P, S], U8, name="xq_scales", align_bytes=64)
        nc.vector.tensor_copy(xq_scales[:], xs[:].indirect(lists["offs"][:]))
        xq_words = keep.tile([P, S], U32, name="xq_words", align_bytes=64)
        nc.vector.tensor_copy(xq_words[:], xw[:].bitcast(U32).indirect(lists["offs"][:]))

        w_bf = [keep.tile([P, 2, P, PACK], BF16, name=f"w_bf{u}", align_bytes=64) for u in range(2)]
        for v in range(2):
            for u in range(2):
                columns = w_raw[v][:].rearrange("p j (m t) -> p m j t", t=PACK)[:, :, :, 2 * u : 2 * u + 2]
                nc.scalar.copy(w_bf[u][:, :, v * P // 2 : (v + 1) * P // 2, :].rearrange("p t m j -> p m j t"), columns)
        w_words = keep.tile([P, PACK, P], U32, name="w_words", align_bytes=64)
        w_scales = keep.tile([P, PACK, P], U8, name="w_scales", align_bytes=64)
        def quantize_w(t):
            nc.vector.quantize_mx(
                out=w_words[:, t, :].bitcast(FP8X4),
                scales=w_scales[:, t, :],
                in_=w_bf[t // 2][:, t % 2, :, :].rearrange("p m j -> p (m j)"),
            )

        quantize_w(0)
        quantize_w(1)
        quantize_w(2)
        quantize_w(3)
        y_banks = []
        for t in range(PACK):
            bank = psum.tile([P, S], F32, name=f"first{t}")
            nc.tensor.matmul_mx(
                out=bank[:],
                lhsT=w_words[:, t, :].bitcast(FP8X4),
                lhsT_scale=w_scales[:, t, :],
                rhs=xq_words[:].bitcast(FP8X4),
                rhs_scale=xq_scales[:],
                start=True,
                stop=True,
            )
            y_banks.append(bank)

        dealt = {}
        for name in ("ca", "cb"):
            picked = keep.tile([P, C], U8, name=name + "_picked", align_bytes=64)
            nc.vector.tensor_copy(picked[:], xs[:].indirect(lists[name][:]))
            dealt[name] = keep.tile([P, C], U8, name=name + "_scales", align_bytes=64)
            nc.vector.tensor_copy(
                dealt[name][:].bitcast(I32).rearrange("p (t a) -> p t a", t=PACK),
                picked[:].bitcast(I32).rearrange("p (a t) -> p t a", t=PACK),
            )

        def pick_words(name, slot):
            words = keep.tile([P, PACK, C // 16, 4], U32, name=name + "_words", tag=slot, align_bytes=64)
            nc.vector.tensor_copy(words[:].rearrange("p t a e -> p a t e"), xw[:].bitcast(U32).indirect(lists[name][:]))
            return words, dealt[name]

        def quantize_and_score(grouped, words, scales, targets, h, name):
            z_words = keep.tile([P, HALF], U32, name=f"{name}_words{h}", align_bytes=64)
            z_scales = keep.tile([P, HALF], U8, name=f"{name}_scales{h}", align_bytes=64)
            nc.vector.quantize_mx(out=z_words[:].bitcast(FP8X4), scales=z_scales[:], in_=grouped[:])
            for t in range(PACK):
                nc.tensor.matmul_mx(
                    out=targets[t],
                    lhsT=words[:, t, :, :].rearrange("p a e -> p (a e)").bitcast(FP8X4),
                    lhsT_scale=scales[:, t * P : (t + 1) * P],
                    rhs=z_words[:].bitcast(FP8X4),
                    rhs_scale=z_scales[:],
                    start=True,
                    stop=True,
                )

        def interleaved(grouped):
            return grouped[:].rearrange("p (c i t) -> p c t i", i=4, t=PACK)

        def planes(tile):
            return tile[:].rearrange("p t (c i) -> p c t i", i=4)

        identity = keep.tile([P, P], F32, name="identity")
        make_identity(nc, identity[:])
        y_sq = [keep.tile([P, 2 * S], F32, name=f"y_sq{t}") for t in range(PACK)]
        yc_other = [keep.tile([P, 2 * S], F32, name=f"yc_other{t}") for t in range(PACK)]
        a_f3 = [keep.tile([P, 2 * S], F32, name=f"a_f3{t}") for t in range(PACK)]
        b_f5 = [keep.tile([P, 2 * S], F32, name=f"b_f5{t}") for t in range(PACK)]
        z = keep.tile([P, PACK, S], F32, name="z")
        right = keep.tile([P, PACK, S], F32, name="right")
        low, high = slice(0, S), slice(S, 2 * S)

        def halves(tile, h):
            return tile[:, :, cols(h)].rearrange("p t (c i) -> p c t i", i=4)

        def fetch(on_vector, target, looked_up):
            if on_vector:
                nc.vector.tensor_copy(target, looked_up)
            else:
                nc.scalar.activation(target, looked_up, ACT.Copy)

        def y_out(t):
            nc.scalar.activation(y_sq[t][:, high], y_banks[t][:], ACT.Square)
            if t not in CFG["aa"]:
                nc.scalar.copy(y_sq[t][:, low], y_banks[t][:])

        turned = {}

        def sum_squares(t):
            for h in range(2):
                nc.scalar.activation(
                    yc_other[t][:, S + h * HALF : S + (h + 1) * HALF], y_sq[t][:, high].indirect(half_list("n1", h)), ACT.Copy
                )
            if t in CFG["aa"]:
                nc.scalar.copy(y_sq[t][:, low], y_banks[t][:])
            turned[t] = psum.tile([P, S], F32, name=f"second{2 * (t % 2)}")
            for c in range(S // P):
                block = slice(S + c * P, S + (c + 1) * P)
                target = turned[t][:, c * P : (c + 1) * P]
                nc.tensor.matmul(target, y_sq[t][:, block], identity[:], start=True, stop=False, is_transpose=True)
                nc.tensor.matmul(target, yc_other[t][:, block], identity[:], start=False, stop=True, is_transpose=True)

        def z_step(t):
            picked = right[:, CFG["early"], :] if t == 3 and CFG["pk"] else work.tile([P, S], F32, name="picked")[:]
            fetch(t in CFG["n2v"], picked, y_sq[t][:].indirect(lists["n2"][:]))
            inv_turned = work.tile([P, S], F32, name="inv_turned")
            nc.scalar.activation(inv_turned[:], turned[t][:], ACT.Abs_reciprocal_sqrt, bias=0.25)
            inv = psum.tile([P, S], F32, name=f"second{2 * (t % 2) + 1}")
            for c in range(S // P):
                nc.tensor.transpose(inv[:, c * P : (c + 1) * P], inv_turned[:, c * P : (c + 1) * P], identity[:])
            for part in ([cols(0), cols(1)] if t in CFG["sh"] else [low]):
                nc.vector.scalar_tensor_tensor(z[:, t, part], picked[:, part], gain[:, t : t + 1], inv[:, part], ALU.mult, ALU.mult)

        def right_step(t):
            right_fetch(t)
            right_mult(t)

        def right_fetch(t):
            fetch(t in CFG["n5v"], b_f5[t][:, high], yc_other[t][:].indirect(lists["n5"][:]))

        def right_mult(t, part=low):
            offsets = lists["n6"][:, part.start // 16 : part.stop // 16]
            nc.vector.tensor_tensor(right[:, t, part], y_sq[t][:].indirect(offsets), b_f5[t][:, high][:, part], ALU.mult)

        def left_mult(t, left, part=low):
            offsets = lists["n4"][:, part.start // 16 : part.stop // 16]
            nc.vector.tensor_tensor(left[:, t, part], y_sq[t][:].indirect(offsets), a_f3[t][:, high][:, part], ALU.mult)

        def left_step(t, left):
            fetch(t in CFG["n3v"], a_f3[t][:, high], yc_other[t][:].indirect(lists["n3"][:]))

        def weigh(t):
            nc.vector.tensor_scalar(yc_other[t][:, low], y_sq[t][:, low], gain2[:, t : t + 1], 0.75, ALU.mult, ALU.mult)

        if CFG["ca"] < 0:
            ca_words, ca_scales = pick_words("ca", "w_bf0")
        if CFG["cb"] < 0:
            cb_words, cb_scales = pick_words("cb", "w_bf1")
        y_out(0)
        sum_squares(0)
        if CFG["de"]:
            weigh(0)
        for t in range(PACK):
            if t + 1 < PACK:
                y_out(t + 1)
                sum_squares(t + 1)
                if CFG["de"]:
                    weigh(t + 1)
            if CFG["kf"] and t < CFG["early"]:
                right_fetch(t)
            z_step(t)
            if not CFG["de"]:
                weigh(t)
            if CFG["ll"] and 0 < t <= CFG["early"]:
                right_mult(t - 1)
            if t < CFG["early"]:
                if not CFG["kf"]:
                    right_fetch(t)
                if not CFG["ll"]:
                    right_mult(t)
            if t == CFG["ca"]:
                ca_words, ca_scales = pick_words("ca", "w_bf0")
            if t == CFG["cb"]:
                cb_words, cb_scales = pick_words("cb", "w_bf1")

        a_banks = [psum.tile([P, S], F32, name=f"first{t}") for t in range(PACK)]
        z_grouped = [keep.tile([P, HALF * PACK], BF16, name=f"z_grouped{h}", align_bytes=64) for h in range(2)]
        for h in range(2):
            nc.vector.tensor_copy(interleaved(z_grouped[h]), halves(z, h))
        for h in range(2):
            quantize_and_score(z_grouped[h], ca_words, ca_scales, [bank[:, cols(h)] for bank in a_banks], h, "z")
        left = keep.tile([P, PACK, S], F32, name="z" if CFG["lz"] else "left")
        for t in range(PACK):
            if t >= CFG["early"]:
                right_fetch(t)
                if t < CFG["jh"]:
                    right_mult(t)
            left_step(t, left)
            if t < CFG["jh"]:
                left_mult(t, left)
        for t in range(PACK):
            nc.scalar.activation(a_f3[t][:, low], a_banks[t][:], ACT.Copy, scale=0.75 * 0.0625)

        b_parts = {}
        b_banks = [psum.tile([P, S], F32, name=f"second{t}") for t in range(PACK)]
        for h in range(2):
            for t in range(CFG["jh"], PACK):
                if t >= CFG["early"]:
                    right_mult(t, cols(h))
                left_mult(t, left, cols(h))
            z2_grouped = keep.tile([P, HALF * PACK], BF16, name="z2_grouped" if CFG["g1"] else f"z2_grouped{h}", align_bytes=64)
            nc.vector.tensor_tensor(interleaved(z2_grouped), halves(left, h), halves(right, h), ALU.subtract)
            b_parts[h] = [b_banks[2 * h + t // 2][:, cols(t % 2)] for t in range(PACK)]
            quantize_and_score(z2_grouped, cb_words, cb_scales, b_parts[h], h, "z2")
            for t in range(PACK):
                nc.scalar.activation(b_f5[t][:, cols(h)], b_parts[h][t], ACT.Copy, scale=0.0625)

        out_rows = out.rearrange("(a t e) n -> t a e n", t=PACK, e=4)
        a_picked = []
        cross = []
        for t in range(PACK):
            picked = keep.tile([P, S], F32, name=f"a_picked{t}")
            fetch(t in CFG["n7v"], picked[:], a_f3[t][:].indirect(lists["n7"][:]))
            a_picked.append(picked)
            cross.append(keep.tile([P, S], F32, name=f"cross{t}"))
        for h in range(2):
            for t in range(PACK):
                nc.vector.scalar_tensor_tensor(cross[t][:, cols(h)], b_parts[h][t], 0.0625, a_picked[t][:, cols(h)], ALU.mult, ALU.mult)
        for t in range(PACK):
            for part in ([cols(0), cols(1)] if t in CFG["hl"] else [low]):
                width = part.stop - part.start
                offsets = lists["n8"][:, part.start // 16 : part.stop // 16]
                direct = work.tile([P, width], F32, name="direct")
                if t in CFG["n8f"]:
                    nc.vector.tensor_tensor(direct[:], b_f5[t][:].indirect(offsets), a_f3[t][:, part], ALU.mult)
                else:
                    b_picked = work.tile([P, width], F32, name="b_picked", bufs=4)
                    nc.scalar.activation(b_picked[:], b_f5[t][:].indirect(offsets), ACT.Copy)
                    nc.vector.scalar_tensor_tensor(direct[:], a_banks[t][:, part], 0.75 * 0.0625, b_picked[:], ALU.mult, ALU.mult)
                result = work.tile([P, width], F32, name="result", bufs=5)
                (nc.gpsimd if t in CFG["rg"] else nc.vector).tensor_tensor(result[:], direct[:], cross[t][:, part], ALU.subtract)
                nc.sync.dma_start(out_rows[t][:, :, part], result[:])
